import numpy as np
import ml_dtypes


def mxq(x, axis, fmt="e4m3"):
    dtype, down = {"e4m3": (ml_dtypes.float8_e4m3fn, 7), "e5m2": (ml_dtypes.float8_e5m2, 14)}[fmt]
    v = np.moveaxis(np.asarray(x, np.float32).astype(ml_dtypes.bfloat16).astype(np.float64), axis, -1)
    blocks = v.reshape(v.shape[:-1] + (-1, 32))
    amax = np.abs(blocks).max(-1, keepdims=True)
    byte = np.maximum(np.where(amax > 0, np.frexp(amax)[1] - 1 + 127, 0) - down, 1)
    scale = np.exp2(byte - 127.0)
    codes = (blocks / scale).astype(np.float32).astype(dtype).astype(np.float64)
    return np.moveaxis((codes * scale).reshape(v.shape), -1, axis)


WIDE = False


def mx_kscale(k):
    if not WIDE:
        return np.ones(k)
    levels = np.array([10, -10, 5, -5, 0])
    if k % 512:
        return np.exp2(np.random.permutation(np.resize(levels, k // 32))).repeat(32)
    a = np.empty((k // 512, 16))
    for p in range(k // 512):
        a[p, :8] = np.random.permutation(np.resize(levels, 8))
        for g in range(8):
            far = levels[np.abs(levels - a[p, g]) >= 10]
            a[p, g + 8] = far[np.random.randint(len(far))]
    return np.exp2(a.ravel()).repeat(32)


def f64(x):
    return np.asarray(x).astype(np.float64)


def striped(idx):
    return np.tile(idx.reshape(-1, 16).T, (8, 1)).astype(np.uint16)


def unstriped(offs):
    return offs[:16].T.reshape(-1).astype(np.int64)


def striped8(idx):
    return np.concatenate([x.reshape(-1, 16).T for x in idx]).astype(np.uint16)


def runs(offs, k):
    lists = np.stack([offs[16 * r : 16 * r + 16].T.reshape(-1) for r in range(8)]).astype(np.int64)
    return lists[np.arange(k) % 512 // 64]


def pack_weight(w):
    k, n = w.shape
    w = f64(np.asarray(w, np.float32).astype(ml_dtypes.bfloat16)).reshape(k // 32, 32, n)
    amax = np.abs(w).max(1)
    byte = np.clip(np.where(amax > 0, np.frexp(amax)[1] - 1 + 127 - 7, 1), 1, 254)
    scaled = (w * np.exp2(127.0 - byte)[:, None, :]).reshape(k, n).astype(np.float32)
    words = np.ascontiguousarray(scaled.reshape(k // 512, 128, 4, n).transpose(0, 1, 3, 2)).astype(ml_dtypes.float8_e4m3fn).view(np.uint8)
    return words, np.ascontiguousarray(byte.astype(np.uint8).reshape(k // 512, 16, n))


def unpack_weight(words, scales):
    g, p, n, _ = words.shape
    vals = np.ascontiguousarray(words).view(ml_dtypes.float8_e4m3fn).astype(np.float64) * np.repeat(np.exp2(scales.astype(np.float64) - 127.0), 8, axis=1)[..., None]
    return vals.transpose(0, 1, 3, 2).reshape(g * 512, n)

def planes(y):
    n, m = y.shape
    v = y.astype(np.float32).astype(ml_dtypes.bfloat16).astype(np.float64).reshape(n // 32, 32, m)
    top = np.abs(v).max(1)
    byte = np.clip(np.where(top > 0, np.frexp(top)[1] - 1 + 127 - 7, 1), 1, 254)
    codes = (v * np.exp2(127.0 - byte)[:, None, :]).reshape(n, m).astype(np.float32).astype(ml_dtypes.float8_e4m3fn).view(np.uint8)
    words = codes.reshape(n // 512, 128, 4, m).transpose(0, 1, 3, 2)
    return np.ascontiguousarray(words), np.ascontiguousarray(byte.astype(np.uint8).reshape(n // 512, 16, m))


K, T, S, H, C = 512, 2048, 512, 512, 512


def setup_inputs():
    n = np.random.standard_normal
    s = mx_kscale(K)[:, None]
    packed_xT = pack_weight(n((K, T)) * s)
    packed_w1 = pack_weight(n((K, H)) / np.sqrt(K) / s)
    return {
        "x_words": packed_xT[0],
        "x_scales": packed_xT[1],
        "w1_words": packed_w1[0],
        "w1_scales": packed_w1[1],
        "gs": (np.random.uniform(0.5, 1.5, (K, 1)) / s).astype(np.float32),
        "offs": striped(np.random.permutation(T)[:S]),
        "n1": striped8(np.stack([np.random.permutation(S) for _ in range(8)])),
        "ca": striped(np.random.permutation(T)[:C]),
        "cb": striped(np.random.permutation(T)[:C]),
        "n2": striped8(np.stack([np.random.permutation(S) for _ in range(8)])),
        "n3": striped8(np.stack([np.random.permutation(S) for _ in range(8)])),
    }


def reference(x_words, x_scales, w1_words, w1_scales, gs, offs, n1, ca, cb, n2, n3):
    x_ca = unpack_weight(x_words, x_scales)[:, unstriped(ca)]
    xq = unpack_weight(x_words, x_scales)[:, unstriped(offs)]
    y = unpack_weight(w1_words, w1_scales).T @ xq
    z = f64(gs) * (y - (y[np.arange(H)[:, None], runs(n1, H)]))
    zq = mxq(z, 0, "e4m3")
    a = 0.0625 * (x_ca.T @ zq)
    x_cb = unpack_weight(x_words, x_scales)[:, unstriped(cb)]
    b = 0.0625 * (x_cb.T @ zq)
    out_0 = (a - (a[np.arange(C)[:, None], runs(n2, C)])) / (np.abs(b) + np.abs(b[np.arange(C)[:, None], runs(n3, C)]) + 0.5)
    return (out_0,) + planes(out_0)

@@ -1,0 +1,200 @@
+from contextlib import ExitStack
+
+import concourse.mybir as mybir
+
+K, T, S, H, C = 512, 2048, 512, 512, 512
+FLOPS = 2 * K * S * (H + 2 * C)
+
+F32 = mybir.dt.float32
+BF16 = mybir.dt.bfloat16
+I32 = mybir.dt.int32
+U32 = mybir.dt.uint32
+U16 = mybir.dt.uint16
+U8 = mybir.dt.uint8
+FP8X4 = mybir.dt.float8_e4m3fn_x4
+ACT = mybir.ActivationFunctionType
+ALU = mybir.AluOpType
+
+P = 128
+PACK = 4
+LANES = 16
+HALVES = ((0, 256), (256, 512))
+TAIL = ((0, 256), (256, 384), (384, 512))
+
+
+def tile_picked_ccmpnormbdif_none_po_kernel(
+    tc, x_words, x_scales, w1_words, w1_scales, gs, offs, n1, ca, cb, n2, n3, out_0, out_1, out_2
+):
+    nc = tc.nc
+    with ExitStack() as ctx:
+        keep = ctx.enter_context(tc.tile_pool(name="keep", bufs=1))
+        psum = ctx.enter_context(tc.psum_pool(name="psum", bufs=1))
+
+        def sb(name, shape, dtype, tag=None):
+            return keep.tile(shape, dtype, name=name, tag=tag or name, align_bytes=64)
+
+        def load_list(name, src):
+            lst = sb(name, [P, S // LANES], U16)
+            nc.sync.dma_start(lst[:], src)
+            return lst
+
+        def load_words(name, src, width):
+            words = sb(name, [P, width], U32)
+            nc.sync.dma_start(words[:].bitcast(I32), src[0].rearrange("p n t -> p (n t)").bitcast(I32))
+            return words
+
+        def load_scales(plane, src):
+            for q in range(4):
+                nc.sync.dma_start(plane[32 * q : 32 * q + 4, :].bitcast(I32), src[0, 4 * q : 4 * q + 4, :].bitcast(I32))
+
+        def dealt(tile):
+            return tile[:].rearrange("p (t m) -> p m t", t=PACK)
+
+        def undealt(tile):
+            return tile[:].rearrange("p (m t) -> p m t", t=PACK)
+
+        def entries(lst, lo, hi):
+            return lst[:, lo // LANES : hi // LANES]
+
+        def interleave(copy, dst, src):
+            copy(dst[:].rearrange("p (c i) t -> p c t i", i=4), src[:].rearrange("p t (c i) -> p c t i", i=4))
+
+        def product(bank, words, plane, t, rhs, rhs_plane):
+            cols = slice(P * t, P * (t + 1))
+            nc.tensor.matmul_mx(
+                out=bank[:], lhsT=words[:, cols].bitcast(FP8X4), lhsT_scale=plane[:, cols],
+                rhs=rhs[:].bitcast(FP8X4), rhs_scale=rhs_plane[:], start=True, stop=True,
+            )
+
+        x_plane = sb("x_plane", [P, T], U8)
+        nc.vector.memset(x_plane[:].bitcast(I32), 0)
+        w_plane_raw = sb("w_plane_raw", [P, H], U8)
+        nc.vector.memset(w_plane_raw[:].bitcast(I32), 0)
+        half = sb("half", [P, 1], F32)
+        nc.gpsimd.memset(half[:], 0.5)
+        warm = sb("warm", [P, 1], F32)
+        nc.scalar.activation(warm[:], half[:], ACT.Abs_reciprocal_sqrt)
+
+        x_tab = load_words("x_tab", x_words, T)
+        offs_l = load_list("offs_l", offs)
+        load_scales(x_plane, x_scales)
+        w_raw = load_words("w_raw", w1_words, H)
+        load_scales(w_plane_raw, w1_scales)
+        cb_l = load_list("cb_l", cb)
+        gain = sb("gain", [P, PACK], F32)
+        nc.sync.dma_start(gain[:], gs.rearrange("(p t) o -> p (t o)", t=PACK))
+        n1_l = load_list("n1_l", n1)
+        ca_l = load_list("ca_l", ca)
+        n3_l = load_list("n3_l", n3)
+        n2_l = load_list("n2_l", n2)
+
+        xq = sb("xq", [P, S], U32)
+        nc.vector.tensor_copy(xq[:], x_tab[:].indirect(offs_l[:]))
+        xq_plane = sb("xq_plane", [P, S], U8)
+        nc.vector.tensor_copy(xq_plane[:], x_plane[:].indirect(offs_l[:]))
+        w = sb("w", [P, H], U32)
+        nc.vector.tensor_copy(dealt(w), undealt(w_raw))
+        w_plane = sb("w_plane", [P, H], U8)
+        nc.vector.tensor_copy(dealt(w_plane), undealt(w_plane_raw))
+
+        def pick_plane(name, lst, tag):
+            raw = sb(name + "_raw", [P, C], U8, tag=tag)
+            nc.vector.tensor_copy(raw[:], x_plane[:].indirect(lst[:]))
+            plane = sb(name, [P, C], U8)
+            nc.vector.tensor_copy(dealt(plane), undealt(raw))
+            return plane
+
+        def pick_words(name, lst, tag):
+            words = sb(name, [P, C], U32, tag=tag)
+            nc.vector.tensor_copy(dealt(words), x_tab[:].indirect(lst[:]))
+            return words
+
+        xb = pick_words("xb", cb_l, "xb")
+        xb_plane = pick_plane("xb_plane", cb_l, "w_plane_raw")
+
+        zneg = [sb("zneg%d" % i, [P, PACK, hi - lo], F32) for i, (lo, hi) in enumerate(TAIL)]
+        for t in range(PACK):
+            bank = psum.tile([P, S], F32, name="y%d" % t, tag="bank%d" % t)
+            product(bank, w, w_plane, t, xq, xq_plane)
+            win = sb("ywin%d" % t, [P, S], F32)
+            own = sb("yown%d" % t, [P, S], F32)
+            nc.scalar.activation(win[:], bank[:], ACT.Copy, scale=gain[:, t : t + 1])
+            nc.scalar.activation(own[:], bank[:], ACT.Copy, scale=gain[:, t : t + 1])
+            for i, (lo, hi) in enumerate(TAIL):
+                nc.vector.tensor_tensor(zneg[i][:, t, :], win[:].indirect(entries(n1_l, lo, hi)), own[:, lo:hi], ALU.subtract)
+
+        zq = sb("zq", [P, S], U32)
+        zq_plane = sb("zq_plane", [P, S], U8)
+        zb = [sb("zb%d" % i, [P, hi - lo, PACK], BF16) for i, (lo, hi) in enumerate(TAIL)]
+        for i in range(len(TAIL)):
+            interleave(nc.vector.tensor_copy if i == len(TAIL) - 1 else nc.scalar.copy, zb[i], zneg[i])
+        for i, (lo, hi) in enumerate(TAIL):
+            nc.vector.quantize_mx(out=zq[:, lo:hi].bitcast(FP8X4), scales=zq_plane[:, lo:hi], in_=zb[i][:].rearrange("p c t -> p (c t)"))
+
+        xa = pick_words("xa", ca_l, "ywin%d" % (PACK - 1))
+        xa_plane = pick_plane("xa_plane", ca_l, "zb1")
+
+        den, awin, aown = [], [], []
+
+        def make_b(t):
+            bank = psum.tile([P, S], F32, name="b%d" % t, tag="bank%d" % (PACK + t))
+            product(bank, xb, xb_plane, t, zq, zq_plane)
+            win = sb("bwin%d" % t, [P, S], F32)
+            own = sb("bown%d" % t, [P, S], F32)
+            nc.scalar.activation(win[:], bank[:], ACT.Abs, scale=0.0625)
+            nc.scalar.activation(own[:], bank[:], ACT.Abs, scale=0.0625)
+            d = sb("den%d" % t, [P, S], F32)
+            for lo, hi in HALVES:
+                nc.vector.tensor_tensor(d[:, lo:hi], win[:].indirect(entries(n3_l, lo, hi)), own[:, lo:hi], ALU.add)
+            den.append(d)
+
+        def make_a(t):
+            bank = psum.tile([P, S], F32, name="a%d" % t, tag="bank%d" % t)
+            product(bank, xa, xa_plane, t, zq, zq_plane)
+            win = sb("awin%d" % t, [P, S], F32)
+            own = sb("aown%d" % t, [P, S], F32)
+            nc.scalar.activation(win[:], bank[:], ACT.Copy, scale=0.0625)
+            nc.sync.dma_start(own[:], win[:])
+            awin.append(win)
+            aown.append(own)
+
+        make_b(0)
+        for t in range(1, PACK):
+            make_b(t)
+            make_a(t - 1)
+        make_a(PACK - 1)
+
+        res = [sb("res%d" % i, [P, PACK, hi - lo], F32) for i, (lo, hi) in enumerate(TAIL)]
+        rows = out_0.rearrange("(p t) s -> p t s", t=PACK)
+        oq = sb("oq", [P, S], U32)
+        oq_plane = sb("oq_plane", [P, S], U8)
+        codes = out_1[0].rearrange("p n t -> p (n t)").bitcast(I32)
+        for t in range(PACK):
+            root = sb("root%d" % t, [P, S], F32)
+            nc.scalar.activation(root[:], den[t][:], ACT.Abs_reciprocal_sqrt, bias=half[:])
+            rec = sb("rec%d" % t, [P, S], F32)
+            nc.scalar.activation(rec[:], root[:], ACT.Square)
+            num = sb("num%d" % t, [P, S], F32)
+
+            def difference(i):
+                lo, hi = TAIL[i]
+                nc.vector.tensor_tensor(num[:, lo:hi], awin[t][:].indirect(entries(n2_l, lo, hi)), aown[t][:, lo:hi], ALU.subtract)
+
+            difference(0)
+            for i, (lo, hi) in enumerate(TAIL):
+                if i + 1 < len(TAIL):
+                    difference(i + 1)
+                nc.vector.tensor_tensor(res[i][:, t, :], num[:, lo:hi], rec[:, lo:hi], ALU.mult)
+                if t == PACK - 2:
+                    nc.sync.dma_start(rows[:, : PACK - 1, lo:hi], res[i][:, : PACK - 1, :])
+                if t == PACK - 1:
+                    nc.sync.dma_start(rows[:, t, lo:hi], res[i][:, t, :])
+        ob = [sb("ob%d" % i, [P, hi - lo, PACK], BF16) for i, (lo, hi) in enumerate(TAIL)]
+        for i in range(len(TAIL)):
+            interleave(nc.vector.tensor_copy if i else nc.scalar.copy, ob[i], res[i])
+        for i, (lo, hi) in enumerate(TAIL):
+            nc.vector.quantize_mx(out=oq[:, lo:hi].bitcast(FP8X4), scales=oq_plane[:, lo:hi], in_=ob[i][:].rearrange("p c t -> p (c t)"))
+            nc.sync.dma_start(codes[:, lo:hi], oq[:, lo:hi].bitcast(I32))
+        for q in range(4):
+            queue = nc.scalar if q % 2 else nc.sync
+            queue.dma_start(out_2[0, 4 * q : 4 * q + 4, :].bitcast(I32), oq_plane[32 * q : 32 * q + 4, :].bitcast(I32))

@@ -19,7 +19,7 @@ P = 128
 PACK = 4
 LANES = 16
 HALVES = ((0, 256), (256, 512))
-TAIL = ((0, 256), (256, 384), (384, 512))
+WHOLE = ((0, 512),)
 
 
 def tile_picked_ccmpnormbdif_none_po_kernel(
@@ -50,14 +50,11 @@ def tile_picked_ccmpnormbdif_none_po_kernel(
         def dealt(tile):
             return tile[:].rearrange("p (t m) -> p m t", t=PACK)
 
-        def undealt(tile):
-            return tile[:].rearrange("p (m t) -> p m t", t=PACK)
-
         def entries(lst, lo, hi):
             return lst[:, lo // LANES : hi // LANES]
 
         def interleave(copy, dst, src):
-            copy(dst[:].rearrange("p (c i) t -> p c t i", i=4), src[:].rearrange("p t (c i) -> p c t i", i=4))
+            copy(dst.rearrange("p (c i) t -> p c t i", i=4), src.rearrange("p t (c i) -> p c t i", i=4))
 
         def product(bank, words, plane, t, rhs, rhs_plane):
             cols = slice(P * t, P * (t + 1))
@@ -88,75 +85,75 @@ def tile_picked_ccmpnormbdif_none_po_kernel(
         n3_l = load_list("n3_l", n3)
         n2_l = load_list("n2_l", n2)
 
-        xq = sb("xq", [P, S], U32)
-        nc.vector.tensor_copy(xq[:], x_tab[:].indirect(offs_l[:]))
-        xq_plane = sb("xq_plane", [P, S], U8)
-        nc.vector.tensor_copy(xq_plane[:], x_plane[:].indirect(offs_l[:]))
-        w = sb("w", [P, H], U32)
-        nc.vector.tensor_copy(dealt(w), undealt(w_raw))
-        w_plane = sb("w_plane", [P, H], U8)
-        nc.vector.tensor_copy(dealt(w_plane), undealt(w_plane_raw))
-
         def pick_plane(name, lst, tag):
-            raw = sb(name + "_raw", [P, C], U8, tag=tag)
-            nc.vector.tensor_copy(raw[:], x_plane[:].indirect(lst[:]))
-            plane = sb(name, [P, C], U8)
-            nc.vector.tensor_copy(dealt(plane), undealt(raw))
+            plane = sb(name, [P, S], U8, tag=tag)
+            nc.vector.tensor_copy(plane[:], x_plane[:].indirect(lst[:]))
             return plane
 
-        def pick_words(name, lst, tag):
+        def deal_plane(name, raw, tag):
+            plane = sb(name, [P, C], U8, tag=tag)
+            nc.vector.tensor_copy(plane[:].rearrange("p (t m) -> p t m", t=PACK), raw[:].rearrange("p (m t) -> p t m", t=PACK))
+            return plane
+
+        def pick_dealt_words(name, lst, tag):
             words = sb(name, [P, C], U32, tag=tag)
             nc.vector.tensor_copy(dealt(words), x_tab[:].indirect(lst[:]))
             return words
 
-        xb = pick_words("xb", cb_l, "xb")
-        xb_plane = pick_plane("xb_plane", cb_l, "w_plane_raw")
+        xq = sb("xq", [P, S], U32)
+        nc.vector.tensor_copy(xq[:], x_tab[:].indirect(offs_l[:]))
+        w = sb("w", [P, H], U32)
+        nc.vector.tensor_copy(w[:].rearrange("p (t c i) -> p c t i", t=PACK, i=4), w_raw[:].rearrange("p (c i t) -> p c t i", t=PACK, i=4))
+        xq_plane = pick_plane("xq_plane", offs_l, "xq_plane")
+        w_plane = deal_plane("w_plane", w_plane_raw, "w_plane")
+        xb = pick_dealt_words("xb", cb_l, "xb")
+        xb_raw = pick_plane("xb_raw", cb_l, "w_plane_raw")
+        xb_plane = deal_plane("xb_plane", xb_raw, "xb_plane")
 
-        zneg = [sb("zneg%d" % i, [P, PACK, hi - lo], F32) for i, (lo, hi) in enumerate(TAIL)]
+        wins = [sb("win0", [P, S], F32)] + [sb("win%d" % r, [P, 2 * S], F32) for r in range(1, 3 * PACK)]
+        last_own = sb("last_own", [P, S], F32)
+        owns = [win[:, S:] for win in wins[1:]] + [last_own[:]]
+
+        def look_up(dst, r, lst, op, cuts):
+            for lo, hi in cuts:
+                nc.vector.tensor_tensor(dst[:, lo:hi], wins[r][:].indirect(entries(lst, lo, hi)), owns[r][:, lo:hi], op)
+
+        zneg = sb("zneg", [P, PACK, S], F32)
         for t in range(PACK):
             bank = psum.tile([P, S], F32, name="y%d" % t, tag="bank%d" % t)
             product(bank, w, w_plane, t, xq, xq_plane)
-            win = sb("ywin%d" % t, [P, S], F32)
-            own = sb("yown%d" % t, [P, S], F32)
-            nc.scalar.activation(win[:], bank[:], ACT.Copy, scale=gain[:, t : t + 1])
-            nc.scalar.activation(own[:], bank[:], ACT.Copy, scale=gain[:, t : t + 1])
-            for i, (lo, hi) in enumerate(TAIL):
-                nc.vector.tensor_tensor(zneg[i][:, t, :], win[:].indirect(entries(n1_l, lo, hi)), own[:, lo:hi], ALU.subtract)
+            nc.scalar.activation(wins[t][:, :S], bank[:], ACT.Copy, scale=gain[:, t : t + 1])
+            nc.scalar.activation(owns[t], bank[:], ACT.Copy, scale=gain[:, t : t + 1])
+            look_up(zneg[:, t, :], t, n1_l, ALU.subtract, HALVES if t in (0, PACK - 1) else WHOLE)
 
         zq = sb("zq", [P, S], U32)
         zq_plane = sb("zq_plane", [P, S], U8)
-        zb = [sb("zb%d" % i, [P, hi - lo, PACK], BF16) for i, (lo, hi) in enumerate(TAIL)]
-        for i in range(len(TAIL)):
-            interleave(nc.vector.tensor_copy if i == len(TAIL) - 1 else nc.scalar.copy, zb[i], zneg[i])
-        for i, (lo, hi) in enumerate(TAIL):
+        zb = [sb("zb%d" % i, [P, hi - lo, PACK], BF16) for i, (lo, hi) in enumerate(HALVES)]
+        interleave(nc.scalar.copy, zb[0][:], zneg[:, :, 0:256])
+        interleave(nc.scalar.copy, zb[1][:, 0:64, :], zneg[:, :, 256:320])
+        interleave(nc.vector.tensor_copy, zb[1][:, 64:256, :], zneg[:, :, 320:512])
+        for i, (lo, hi) in enumerate(HALVES):
             nc.vector.quantize_mx(out=zq[:, lo:hi].bitcast(FP8X4), scales=zq_plane[:, lo:hi], in_=zb[i][:].rearrange("p c t -> p (c t)"))
+        xa_raw = pick_plane("xa_raw", ca_l, "zneg")
+        xa = pick_dealt_words("xa", ca_l, "zb1")
+        xa_plane = deal_plane("xa_plane", xa_raw, "xa_plane")
 
-        xa = pick_words("xa", ca_l, "ywin%d" % (PACK - 1))
-        xa_plane = pick_plane("xa_plane", ca_l, "zb1")
-
-        den, awin, aown = [], [], []
+        den = [sb("den%d" % t, [P, S], F32) for t in range(PACK)]
 
         def make_b(t):
-            bank = psum.tile([P, S], F32, name="b%d" % t, tag="bank%d" % (PACK + t))
+            r = PACK + t
+            bank = psum.tile([P, S], F32, name="b%d" % t, tag="bank%d" % r)
             product(bank, xb, xb_plane, t, zq, zq_plane)
-            win = sb("bwin%d" % t, [P, S], F32)
-            own = sb("bown%d" % t, [P, S], F32)
-            nc.scalar.activation(win[:], bank[:], ACT.Abs, scale=0.0625)
-            nc.scalar.activation(own[:], bank[:], ACT.Abs, scale=0.0625)
-            d = sb("den%d" % t, [P, S], F32)
-            for lo, hi in HALVES:
-                nc.vector.tensor_tensor(d[:, lo:hi], win[:].indirect(entries(n3_l, lo, hi)), own[:, lo:hi], ALU.add)
-            den.append(d)
+            nc.scalar.activation(wins[r][:, :S], bank[:], ACT.Abs, scale=0.0625)
+            nc.scalar.activation(owns[r], bank[:], ACT.Abs, scale=0.0625)
+            look_up(den[t], r, n3_l, ALU.add, WHOLE)
 
         def make_a(t):
+            r = 2 * PACK + t
             bank = psum.tile([P, S], F32, name="a%d" % t, tag="bank%d" % t)
             product(bank, xa, xa_plane, t, zq, zq_plane)
-            win = sb("awin%d" % t, [P, S], F32)
-            own = sb("aown%d" % t, [P, S], F32)
-            nc.scalar.activation(win[:], bank[:], ACT.Copy, scale=0.0625)
-            nc.sync.dma_start(own[:], win[:])
-            awin.append(win)
-            aown.append(own)
+            nc.scalar.activation(wins[r][:, :S], bank[:], ACT.Copy, scale=0.0625)
+            nc.sync.dma_start(owns[r], wins[r][:, :S])
 
         make_b(0)
         for t in range(1, PACK):
@@ -164,35 +161,31 @@ def tile_picked_ccmpnormbdif_none_po_kernel(
             make_a(t - 1)
         make_a(PACK - 1)
 
-        res = [sb("res%d" % i, [P, PACK, hi - lo], F32) for i, (lo, hi) in enumerate(TAIL)]
+        res = sb("res", [P, PACK, S], F32)
         rows = out_0.rearrange("(p t) s -> p t s", t=PACK)
         oq = sb("oq", [P, S], U32)
         oq_plane = sb("oq_plane", [P, S], U8)
         codes = out_1[0].rearrange("p n t -> p (n t)").bitcast(I32)
+        num = [sb("num%d" % t, [P, S], F32) for t in range(PACK)]
+        rec = [sb("rec%d" % t, [P, S], F32) for t in range(PACK)]
+
+        def quotient(t, cuts):
+            for lo, hi in cuts:
+                nc.vector.tensor_tensor(res[:, t, lo:hi], num[t][:, lo:hi], rec[t][:, lo:hi], ALU.mult)
+                nc.sync.dma_start(rows[:, t, lo:hi], res[:, t, lo:hi])
+
         for t in range(PACK):
             root = sb("root%d" % t, [P, S], F32)
             nc.scalar.activation(root[:], den[t][:], ACT.Abs_reciprocal_sqrt, bias=half[:])
-            rec = sb("rec%d" % t, [P, S], F32)
-            nc.scalar.activation(rec[:], root[:], ACT.Square)
-            num = sb("num%d" % t, [P, S], F32)
-
-            def difference(i):
-                lo, hi = TAIL[i]
-                nc.vector.tensor_tensor(num[:, lo:hi], awin[t][:].indirect(entries(n2_l, lo, hi)), aown[t][:, lo:hi], ALU.subtract)
-
-            difference(0)
-            for i, (lo, hi) in enumerate(TAIL):
-                if i + 1 < len(TAIL):
-                    difference(i + 1)
-                nc.vector.tensor_tensor(res[i][:, t, :], num[:, lo:hi], rec[:, lo:hi], ALU.mult)
-                if t == PACK - 2:
-                    nc.sync.dma_start(rows[:, : PACK - 1, lo:hi], res[i][:, : PACK - 1, :])
-                if t == PACK - 1:
-                    nc.sync.dma_start(rows[:, t, lo:hi], res[i][:, t, :])
-        ob = [sb("ob%d" % i, [P, hi - lo, PACK], BF16) for i, (lo, hi) in enumerate(TAIL)]
-        for i in range(len(TAIL)):
-            interleave(nc.vector.tensor_copy if i else nc.scalar.copy, ob[i], res[i])
-        for i, (lo, hi) in enumerate(TAIL):
+            nc.scalar.activation(rec[t][:], root[:], ACT.Square)
+            look_up(num[t], 2 * PACK + t, n2_l, ALU.subtract, HALVES if t == PACK - 1 else WHOLE)
+            if t:
+                quotient(t - 1, WHOLE)
+        quotient(PACK - 1, HALVES)
+        ob = [sb("ob%d" % i, [P, hi - lo, PACK], BF16) for i, (lo, hi) in enumerate(HALVES)]
+        for i, (lo, hi) in enumerate(HALVES):
+            interleave(nc.vector.tensor_copy if i else nc.scalar.copy, ob[i][:], res[:, :, lo:hi])
+        for i, (lo, hi) in enumerate(HALVES):
             nc.vector.quantize_mx(out=oq[:, lo:hi].bitcast(FP8X4), scales=oq_plane[:, lo:hi], in_=ob[i][:].rearrange("p c t -> p (c t)"))
             nc.sync.dma_start(codes[:, lo:hi], oq[:, lo:hi].bitcast(I32))
         for q in range(4):

@@ -63,24 +63,26 @@ def tile_picked_ccmpnormbdif_none_po_kernel(
                 rhs=rhs[:].bitcast(FP8X4), rhs_scale=rhs_plane[:], start=True, stop=True,
             )
 
-        x_plane = sb("x_plane", [P, T], U8)
-        nc.vector.memset(x_plane[:].bitcast(I32), 0)
         w_plane_raw = sb("w_plane_raw", [P, H], U8)
         nc.vector.memset(w_plane_raw[:].bitcast(I32), 0)
+        x_plane = sb("x_plane", [P, T], U8)
+        nc.vector.memset(x_plane[:].bitcast(I32), 0)
         half = sb("half", [P, 1], F32)
         nc.gpsimd.memset(half[:], 0.5)
         warm = sb("warm", [P, 1], F32)
         nc.scalar.activation(warm[:], half[:], ACT.Abs_reciprocal_sqrt)
 
-        x_tab = load_words("x_tab", x_words, T)
+        x_rows = sb("x_rows", [P, T], U8)
+        load_scales(x_rows, x_scales)
         offs_l = load_list("offs_l", offs)
-        load_scales(x_plane, x_scales)
+        x_tab = load_words("x_tab", x_words, T)
+        w_rows = sb("w_rows", [P, H], U8)
+        load_scales(w_rows, w1_scales)
         w_raw = load_words("w_raw", w1_words, H)
-        load_scales(w_plane_raw, w1_scales)
-        cb_l = load_list("cb_l", cb)
         gain = sb("gain", [P, PACK], F32)
         nc.sync.dma_start(gain[:], gs.rearrange("(p t) o -> p (t o)", t=PACK))
         n1_l = load_list("n1_l", n1)
+        cb_l = load_list("cb_l", cb)
         ca_l = load_list("ca_l", ca)
         n3_l = load_list("n3_l", n3)
         n2_l = load_list("n2_l", n2)
@@ -100,14 +102,18 @@ def tile_picked_ccmpnormbdif_none_po_kernel(
             nc.vector.tensor_copy(dealt(words), x_tab[:].indirect(lst[:]))
             return words
 
+        for q in range(4):
+            live = slice(32 * q, 32 * q + 4)
+            nc.vector.tensor_copy(x_plane[live, :].bitcast(I32), x_rows[live, :].bitcast(I32))
+            nc.gpsimd.tensor_copy(w_plane_raw[live, :].bitcast(I32), w_rows[live, :].bitcast(I32))
+        xq_plane = pick_plane("xq_plane", offs_l, "xq_plane")
         xq = sb("xq", [P, S], U32)
         nc.vector.tensor_copy(xq[:], x_tab[:].indirect(offs_l[:]))
         w = sb("w", [P, H], U32)
         nc.vector.tensor_copy(w[:].rearrange("p (t c i) -> p c t i", t=PACK, i=4), w_raw[:].rearrange("p (c i t) -> p c t i", t=PACK, i=4))
-        xq_plane = pick_plane("xq_plane", offs_l, "xq_plane")
         w_plane = deal_plane("w_plane", w_plane_raw, "w_plane")
+        xb_raw = pick_plane("xb_raw", cb_l, "xb_raw")
         xb = pick_dealt_words("xb", cb_l, "xb")
-        xb_raw = pick_plane("xb_raw", cb_l, "w_plane_raw")
         xb_plane = deal_plane("xb_plane", xb_raw, "xb_plane")
 
         wins = [sb("win0", [P, S], F32)] + [sb("win%d" % r, [P, 2 * S], F32) for r in range(1, 3 * PACK)]

@@ -146,26 +146,31 @@ def tile_picked_ccmpnormbdif_none_po_kernel(
 
         den = [sb("den%d" % t, [P, S], F32) for t in range(PACK)]
 
-        def make_b(t):
+        b_bank = [psum.tile([P, S], F32, name="b%d" % t, tag="bank%d" % (PACK + t)) for t in range(PACK)]
+        a_bank = [psum.tile([P, S], F32, name="a%d" % t, tag="bank%d" % t) for t in range(PACK)]
+        for t in range(PACK):
+            product(b_bank[t], xb, xb_plane, t, zq, zq_plane)
+        for t in range(PACK):
+            product(a_bank[t], xa, xa_plane, t, zq, zq_plane)
+
+        def leave_b(t):
             r = PACK + t
-            bank = psum.tile([P, S], F32, name="b%d" % t, tag="bank%d" % r)
-            product(bank, xb, xb_plane, t, zq, zq_plane)
-            nc.scalar.activation(wins[r][:, :S], bank[:], ACT.Abs, scale=0.0625)
-            nc.scalar.activation(owns[r], bank[:], ACT.Abs, scale=0.0625)
+            nc.scalar.activation(wins[r][:, :S], b_bank[t][:], ACT.Abs, scale=0.0625)
+            nc.scalar.activation(owns[r], b_bank[t][:], ACT.Abs, scale=0.0625)
             look_up(den[t], r, n3_l, ALU.add, WHOLE)
 
-        def make_a(t):
+        def leave_a(t):
             r = 2 * PACK + t
-            bank = psum.tile([P, S], F32, name="a%d" % t, tag="bank%d" % t)
-            product(bank, xa, xa_plane, t, zq, zq_plane)
-            nc.scalar.activation(wins[r][:, :S], bank[:], ACT.Copy, scale=0.0625)
+            nc.scalar.activation(wins[r][:, :S], a_bank[t][:], ACT.Copy, scale=0.0625)
             nc.sync.dma_start(owns[r], wins[r][:, :S])
 
-        make_b(0)
-        for t in range(1, PACK):
-            make_b(t)
-            make_a(t - 1)
-        make_a(PACK - 1)
+        for t in range(PACK - 1):
+            leave_b(t)
+        for t in range(PACK // 2):
+            leave_a(t)
+        leave_b(PACK - 1)
+        for t in range(PACK // 2, PACK):
+            leave_a(t)
 
         res = sb("res", [P, PACK, S], F32)
         rows = out_0.rearrange("(p t) s -> p t s", t=PACK)

from contextlib import ExitStack

import concourse.mybir as mybir

K, T, S, H, C = 512, 2048, 512, 512, 512
FLOPS = 2 * K * S * (H + 2 * C)

F32 = mybir.dt.float32
BF16 = mybir.dt.bfloat16
I32 = mybir.dt.int32
U32 = mybir.dt.uint32
U16 = mybir.dt.uint16
U8 = mybir.dt.uint8
FP8X4 = mybir.dt.float8_e4m3fn_x4
ACT = mybir.ActivationFunctionType
ALU = mybir.AluOpType

P = 128
PACK = 4
LANES = 16
HALVES = ((0, 256), (256, 512))
WHOLE = ((0, 512),)


def tile_picked_ccmpnormbdif_none_po_kernel(
    tc, x_words, x_scales, w1_words, w1_scales, gs, offs, n1, ca, cb, n2, n3, out_0, out_1, out_2
):
    nc = tc.nc
    with ExitStack() as ctx:
        keep = ctx.enter_context(tc.tile_pool(name="keep", bufs=1))
        psum = ctx.enter_context(tc.psum_pool(name="psum", bufs=1))

        def sb(name, shape, dtype, tag=None):
            return keep.tile(shape, dtype, name=name, tag=tag or name, align_bytes=64)

        def load_list(name, src):
            lst = sb(name, [P, S // LANES], U16)
            nc.sync.dma_start(lst[:], src)
            return lst

        def load_words(name, src, width):
            words = sb(name, [P, width], U32)
            nc.sync.dma_start(words[:].bitcast(I32), src[0].rearrange("p n t -> p (n t)").bitcast(I32))
            return words

        def load_scales(plane, src):
            for q in range(4):
                nc.sync.dma_start(plane[32 * q : 32 * q + 4, :].bitcast(I32), src[0, 4 * q : 4 * q + 4, :].bitcast(I32))

        def dealt(tile):
            return tile[:].rearrange("p (t m) -> p m t", t=PACK)

        def entries(lst, lo, hi):
            return lst[:, lo // LANES : hi // LANES]

        def interleave(copy, dst, src):
            copy(dst.rearrange("p (c i) t -> p c t i", i=4), src.rearrange("p t (c i) -> p c t i", i=4))

        def product(bank, words, plane, t, rhs, rhs_plane):
            cols = slice(P * t, P * (t + 1))
            nc.tensor.matmul_mx(
                out=bank[:], lhsT=words[:, cols].bitcast(FP8X4), lhsT_scale=plane[:, cols],
                rhs=rhs[:].bitcast(FP8X4), rhs_scale=rhs_plane[:], start=True, stop=True,
            )

        w_plane_raw = sb("w_plane_raw", [P, H], U8)
        nc.vector.memset(w_plane_raw[:].bitcast(I32), 0)
        x_plane = sb("x_plane", [P, T], U8)
        nc.vector.memset(x_plane[:].bitcast(I32), 0)
        half = sb("half", [P, 1], F32)
        nc.gpsimd.memset(half[:], 0.5)
        warm = sb("warm", [P, 1], F32)
        nc.scalar.activation(warm[:], half[:], ACT.Abs_reciprocal_sqrt)

        x_rows = sb("x_rows", [P, T], U8)
        load_scales(x_rows, x_scales)
        offs_l = load_list("offs_l", offs)
        x_tab = load_words("x_tab", x_words, T)
        w_rows = sb("w_rows", [P, H], U8)
        load_scales(w_rows, w1_scales)
        w_raw = load_words("w_raw", w1_words, H)
        gain = sb("gain", [P, PACK], F32)
        nc.sync.dma_start(gain[:], gs.rearrange("(p t) o -> p (t o)", t=PACK))
        n1_l = load_list("n1_l", n1)
        cb_l = load_list("cb_l", cb)
        ca_l = load_list("ca_l", ca)
        n3_l = load_list("n3_l", n3)
        n2_l = load_list("n2_l", n2)

        def pick_plane(name, lst, tag):
            plane = sb(name, [P, S], U8, tag=tag)
            nc.vector.tensor_copy(plane[:], x_plane[:].indirect(lst[:]))
            return plane

        def deal_plane(name, raw, tag):
            plane = sb(name, [P, C], U8, tag=tag)
            nc.vector.tensor_copy(plane[:].rearrange("p (t m) -> p t m", t=PACK), raw[:].rearrange("p (m t) -> p t m", t=PACK))
            return plane

        def pick_dealt_words(name, lst, tag):
            words = sb(name, [P, C], U32, tag=tag)
            nc.vector.tensor_copy(dealt(words), x_tab[:].indirect(lst[:]))
            return words

        for q in range(4):
            live = slice(32 * q, 32 * q + 4)
            nc.vector.tensor_copy(x_plane[live, :].bitcast(I32), x_rows[live, :].bitcast(I32))
            nc.gpsimd.tensor_copy(w_plane_raw[live, :].bitcast(I32), w_rows[live, :].bitcast(I32))
        xq_plane = pick_plane("xq_plane", offs_l, "xq_plane")
        xq = sb("xq", [P, S], U32)
        nc.vector.tensor_copy(xq[:], x_tab[:].indirect(offs_l[:]))
        w = sb("w", [P, H], U32)
        nc.vector.tensor_copy(w[:].rearrange("p (t c i) -> p c t i", t=PACK, i=4), w_raw[:].rearrange("p (c i t) -> p c t i", t=PACK, i=4))
        w_plane = deal_plane("w_plane", w_plane_raw, "w_plane")
        xb_raw = pick_plane("xb_raw", cb_l, "xb_raw")
        xb = pick_dealt_words("xb", cb_l, "xb")
        xb_plane = deal_plane("xb_plane", xb_raw, "xb_plane")

        wins = [sb("win0", [P, S], F32)] + [sb("win%d" % r, [P, 2 * S], F32) for r in range(1, 3 * PACK)]
        last_own = sb("last_own", [P, S], F32)
        owns = [win[:, S:] for win in wins[1:]] + [last_own[:]]

        def look_up(dst, r, lst, op, cuts):
            for lo, hi in cuts:
                nc.vector.tensor_tensor(dst[:, lo:hi], wins[r][:].indirect(entries(lst, lo, hi)), owns[r][:, lo:hi], op)

        zneg = sb("zneg", [P, PACK, S], F32)
        for t in range(PACK):
            bank = psum.tile([P, S], F32, name="y%d" % t, tag="bank%d" % t)
            product(bank, w, w_plane, t, xq, xq_plane)
            nc.scalar.activation(wins[t][:, :S], bank[:], ACT.Copy, scale=gain[:, t : t + 1])
            nc.scalar.activation(owns[t], bank[:], ACT.Copy, scale=gain[:, t : t + 1])
            look_up(zneg[:, t, :], t, n1_l, ALU.subtract, HALVES if t in (0, PACK - 1) else WHOLE)

        zq = sb("zq", [P, S], U32)
        zq_plane = sb("zq_plane", [P, S], U8)
        zb = [sb("zb%d" % i, [P, hi - lo, PACK], BF16) for i, (lo, hi) in enumerate(HALVES)]
        interleave(nc.scalar.copy, zb[0][:], zneg[:, :, 0:256])
        interleave(nc.scalar.copy, zb[1][:, 0:64, :], zneg[:, :, 256:320])
        interleave(nc.vector.tensor_copy, zb[1][:, 64:256, :], zneg[:, :, 320:512])
        for i, (lo, hi) in enumerate(HALVES):
            nc.vector.quantize_mx(out=zq[:, lo:hi].bitcast(FP8X4), scales=zq_plane[:, lo:hi], in_=zb[i][:].rearrange("p c t -> p (c t)"))
        xa_raw = pick_plane("xa_raw", ca_l, "zneg")
        xa = pick_dealt_words("xa", ca_l, "zb1")
        xa_plane = deal_plane("xa_plane", xa_raw, "xa_plane")

        den = [sb("den%d" % t, [P, S], F32) for t in range(PACK)]

        b_bank = [psum.tile([P, S], F32, name="b%d" % t, tag="bank%d" % (PACK + t)) for t in range(PACK)]
        a_bank = [psum.tile([P, S], F32, name="a%d" % t, tag="bank%d" % t) for t in range(PACK)]
        for t in range(PACK):
            product(b_bank[t], xb, xb_plane, t, zq, zq_plane)
        for t in range(PACK):
            product(a_bank[t], xa, xa_plane, t, zq, zq_plane)

        def leave_b(t):
            r = PACK + t
            nc.scalar.activation(wins[r][:, :S], b_bank[t][:], ACT.Abs, scale=0.0625)
            nc.scalar.activation(owns[r], b_bank[t][:], ACT.Abs, scale=0.0625)
            look_up(den[t], r, n3_l, ALU.add, WHOLE)

        def leave_a(t):
            r = 2 * PACK + t
            nc.scalar.activation(wins[r][:, :S], a_bank[t][:], ACT.Copy, scale=0.0625)
            nc.sync.dma_start(owns[r], wins[r][:, :S])

        for t in range(PACK - 1):
            leave_b(t)
        for t in range(PACK // 2):
            leave_a(t)
        leave_b(PACK - 1)
        for t in range(PACK // 2, PACK):
            leave_a(t)

        res = sb("res", [P, PACK, S], F32)
        rows = out_0.rearrange("(p t) s -> p t s", t=PACK)
        oq = sb("oq", [P, S], U32)
        oq_plane = sb("oq_plane", [P, S], U8)
        codes = out_1[0].rearrange("p n t -> p (n t)").bitcast(I32)
        num = [sb("num%d" % t, [P, S], F32) for t in range(PACK)]
        rec = [sb("rec%d" % t, [P, S], F32) for t in range(PACK)]

        def quotient(t, cuts):
            for lo, hi in cuts:
                nc.vector.tensor_tensor(res[:, t, lo:hi], num[t][:, lo:hi], rec[t][:, lo:hi], ALU.mult)
                nc.sync.dma_start(rows[:, t, lo:hi], res[:, t, lo:hi])

        for t in range(PACK):
            root = sb("root%d" % t, [P, S], F32)
            nc.scalar.activation(root[:], den[t][:], ACT.Abs_reciprocal_sqrt, bias=half[:])
            nc.scalar.activation(rec[t][:], root[:], ACT.Square)
            look_up(num[t], 2 * PACK + t, n2_l, ALU.subtract, HALVES if t == PACK - 1 else WHOLE)
            if t:
                quotient(t - 1, WHOLE)
        quotient(PACK - 1, HALVES)
        ob = [sb("ob%d" % i, [P, hi - lo, PACK], BF16) for i, (lo, hi) in enumerate(HALVES)]
        for i, (lo, hi) in enumerate(HALVES):
            interleave(nc.vector.tensor_copy if i else nc.scalar.copy, ob[i][:], res[:, :, lo:hi])
        for i, (lo, hi) in enumerate(HALVES):
            nc.vector.quantize_mx(out=oq[:, lo:hi].bitcast(FP8X4), scales=oq_plane[:, lo:hi], in_=ob[i][:].rearrange("p c t -> p (c t)"))
            nc.sync.dma_start(codes[:, lo:hi], oq[:, lo:hi].bitcast(I32))
        for q in range(4):
            queue = nc.scalar if q % 2 else nc.sync
            queue.dma_start(out_2[0, 4 * q : 4 * q + 4, :].bitcast(I32), oq_plane[32 * q : 32 * q + 4, :].bitcast(I32))
